import numpy as np
import ml_dtypes


def mxq(x, axis, fmt="e4m3"):
    dtype, down = {"e4m3": (ml_dtypes.float8_e4m3fn, 7), "e5m2": (ml_dtypes.float8_e5m2, 14)}[fmt]
    v = np.moveaxis(np.asarray(x, np.float32).astype(ml_dtypes.bfloat16).astype(np.float64), axis, -1)
    blocks = v.reshape(v.shape[:-1] + (-1, 32))
    amax = np.abs(blocks).max(-1, keepdims=True)
    byte = np.maximum(np.where(amax > 0, np.frexp(amax)[1] - 1 + 127, 0) - down, 1)
    scale = np.exp2(byte - 127.0)
    codes = (blocks / scale).astype(np.float32).astype(dtype).astype(np.float64)
    return np.moveaxis((codes * scale).reshape(v.shape), -1, axis)


WIDE = False


def mx_kscale(k):
    if not WIDE:
        return np.ones(k)
    levels = np.array([10, -10, 5, -5, 0])
    if k % 512:
        return np.exp2(np.random.permutation(np.resize(levels, k // 32))).repeat(32)
    a = np.empty((k // 512, 16))
    for p in range(k // 512):
        a[p, :8] = np.random.permutation(np.resize(levels, 8))
        for g in range(8):
            far = levels[np.abs(levels - a[p, g]) >= 10]
            a[p, g + 8] = far[np.random.randint(len(far))]
    return np.exp2(a.ravel()).repeat(32)


BF16 = ml_dtypes.bfloat16


def bf(x):
    return np.asarray(x, np.float32).astype(BF16)


def f64(x):
    return np.asarray(x).astype(np.float64)


B, N, F, C = 2, 1024, 512, 256


def erf(v):
    a = np.clip(v, -6.0, 6.0)
    term = a
    total = a
    for n in range(150):
        term = term * (2.0 * a * a / (2 * n + 3))
        total = total + term
    series = 2.0 / np.sqrt(np.pi) * np.exp(-a * a) * total
    return np.where(np.abs(v) <= 6.0, series, np.sign(v))


def gelu_erf(y):
    return 0.5 * y * (1.0 + erf(y / np.sqrt(2.0)))


def centred_assignment(logits):
    num_clusters = logits.shape[-1]
    e = np.exp(logits - logits.max(-1, keepdims=True))
    return num_clusters * (e / e.sum(-1, keepdims=True)) - 1.0


def draw0():
    s = mx_kscale(N)
    u = mx_kscale(N)
    return {"adj": bf(np.random.standard_normal((B, N, N)) / np.sqrt(N) / s[None, None, :]),
            "logits": bf(np.random.standard_normal((B, N, C)) * 0.8),
            "x": bf(np.random.standard_normal((B, N, F)) * s[None, :, None]),
            "gr": bf((1.0 + 0.1 * np.random.standard_normal(N)) * s),
            "gl": bf((1.0 + 0.1 * np.random.standard_normal(N)) * u),
            "go": bf((1.0 + 0.1 * np.random.standard_normal(N)) / u)}


def core(adj, logits, x, gr, gl, go):
    adj, logits, x = f64(adj), f64(logits), f64(x)
    gr, gl, go = f64(gr), f64(gl), f64(go)
    num_nodes = adj.shape[-1]

    a = centred_assignment(logits)

    sr = a * gr[None, :, None]
    sl = a * gl[None, :, None] / np.sqrt(num_nodes)

    adjq = mxq(adj, 2, "e4m3")
    t = adjq @ mxq(x, 1, "e4m3")
    z = gelu_erf(t) * go[None, :, None]

    q = go[None, :, None] * (adjq @ mxq(sr, 1, "e4m3"))

    slq = mxq(sl, 1, "e4m3")
    x_pool = np.swapaxes(slq, 1, 2) @ mxq(z, 1, "e4m3")

    a_pool = np.swapaxes(slq, 1, 2) @ mxq(q, 1, "e4m3")

    return x_pool, a_pool


def e4m3fn_bytes(y):
    return np.clip(np.asarray(y, np.float64), -448.0, 448.0).astype(np.float32).astype(ml_dtypes.float8_e4m3fn).view(np.uint8)


def e4m3fn_values(b):
    return np.asarray(b, np.uint8).view(ml_dtypes.float8_e4m3fn).astype(np.float64)


def setup_inputs():
    d = draw0()
    x0 = np.asarray(d['adj']).astype(np.float64)
    s = (np.max(np.abs(x0), axis=(0, 1), keepdims=True) / 448.0).astype(np.float32)
    out = {}
    for k, v in d.items():
        if k == 'adj':
            out['adj_bytes'] = e4m3fn_bytes(x0 / s.astype(np.float64))
            out['adj_scale'] = s
        else:
            out[k] = v
    return out


def reference(adj_bytes, adj_scale, logits, x, gr, gl, go):
    return core(e4m3fn_values(adj_bytes) * adj_scale.astype(np.float64), logits, x, gr, gl, go)

@@ -1,0 +1,293 @@
+from contextlib import ExitStack
+
+import concourse.mybir as mybir
+from concourse.masks import make_identity
+
+B, N, F, C = 2, 1024, 512, 256
+P = 128
+T = 4
+G = N // (P * T)
+R = G * T
+
+F32 = mybir.dt.float32
+BF16 = mybir.dt.bfloat16
+U32 = mybir.dt.uint32
+U8 = mybir.dt.uint8
+FP8 = mybir.dt.float8_e4m3fn
+FP8X4 = mybir.dt.float8_e4m3fn_x4
+ALU = mybir.AluOpType
+ACT = mybir.ActivationFunctionType
+AX = mybir.AxisListType
+
+FLOPS = 2 * B * (N * N * (F + C) + C * N * (F + C))
+
+
+def tile_diffpoolcoarsen_kernel(tc, adj_bytes, adj_scale, logits, x, gr, gl, go, out_0, out_1):
+    nc = tc.nc
+    with ExitStack() as ctx:
+        sb = ctx.enter_context(tc.tile_pool(name="sb", bufs=1))
+        ps = ctx.enter_context(tc.psum_pool(name="ps", bufs=1))
+
+        ident_f = sb.tile([P, P], F32, name="ident_f", align_bytes=64)
+        make_identity(nc, ident_f[:])
+        ident_b = sb.tile([P, P], BF16, name="ident_b", align_bytes=64)
+        nc.gpsimd.tensor_copy(out=ident_b[:], in_=ident_f[:])
+        warm = sb.tile([P, 1], F32, name="warm")
+        nc.vector.memset(warm[:], 0.0)
+        warm2 = sb.tile([P, 1], F32, name="warm2")
+        nc.scalar.activation(out=warm2[:], in_=warm[:], func=ACT.Exp)
+
+        lg = []
+        raw = {}
+        xs = {}
+
+        def load_logits(b):
+            t = sb.tile([P, G, T, C], BF16, name="lg", bufs=2, align_bytes=64)
+            nc.sync.dma_start(out=t[:], in_=logits[b].rearrange("(g p t) c -> p g t c", p=P, t=T))
+            lg.append(t)
+
+        def load_adj(b, g, split=1):
+            t = sb.tile([P, T, N], U8, name="adj_raw", bufs=4, align_bytes=64)
+            src = adj_bytes[b].rearrange("(g p t) m -> g p t m", p=P, t=T)[g]
+            w = T // split
+            for i in range(split):
+                nc.sync.dma_start(out=t[:, i * w:(i + 1) * w, :], in_=src[:, i * w:(i + 1) * w, :])
+            raw[b, g] = t
+
+        def load_x(b, g):
+            t = sb.tile([P, T, F], BF16, name="xs", bufs=4, align_bytes=64)
+            nc.sync.dma_start(out=t[:], in_=x[b].rearrange("(g p t) f -> g p t f", p=P, t=T)[g])
+            xs[b, g] = t
+
+        gains = {}
+        for nm, src in (("gr", gr), ("gl", gl), ("go", go)):
+            t = sb.tile([P, G, T], BF16, name="gain_" + nm, align_bytes=64)
+            nc.gpsimd.dma_start(out=t[:], in_=src.rearrange("(g p t) -> p g t", p=P, t=T))
+            gains[nm] = t
+
+        load_logits(0)
+        scale_sb = sb.tile([P, N], F32, name="scale_sb", align_bytes=64)
+        nc.sync.dma_start(out=scale_sb[:], in_=adj_scale.rearrange("a b m -> (a b m)").partition_broadcast(P))
+        load_adj(0, 0, split=2)
+        load_logits(1)
+        load_x(0, 0)
+        load_x(0, 1)
+        load_adj(0, 1)
+        load_x(1, 0)
+        load_x(1, 1)
+        load_adj(1, 0)
+        load_adj(1, 1)
+
+        def gain_tile(nm, src, factor):
+            t = sb.tile([P, R], F32, name=nm, align_bytes=64)
+            nc.gpsimd.tensor_scalar(out=t[:], in0=gains[src][:].rearrange("p g t -> p (g t)"), scalar1=factor,
+                                    scalar2=0.0, op0=ALU.mult, op1=ALU.add)
+            return t
+
+        gr256 = gain_tile("gr256", "gr", 256.0)
+        gr_n = gain_tile("gr_n", "gr", -1.0)
+        gl8 = gain_tile("gl8", "gl", 8.0)
+        gl_n = gain_tile("gl_n", "gl", -1.0 / 32.0)
+        go_f = gain_tile("go_f", "go", 1.0)
+
+        e = {}
+        srq, slq = {}, {}
+
+        def softmax_exp(b):
+            l = lg[b][:].rearrange("p g t c -> p (g t) c")
+            m1 = sb.tile([P, R, 128], BF16, name="m1", bufs=2, align_bytes=64)
+            nc.vector.tensor_tensor(out=m1[:], in0=l[:, :, 0:128], in1=l[:, :, 128:256], op=ALU.max)
+            m2 = sb.tile([P, R, 64], BF16, name="m2", bufs=2, align_bytes=64)
+            nc.vector.tensor_tensor(out=m2[:], in0=m1[:, :, 0:64], in1=m1[:, :, 64:128], op=ALU.max)
+            m3 = sb.tile([P, R, 32], BF16, name="m3", bufs=2, align_bytes=64)
+            nc.vector.tensor_tensor(out=m3[:], in0=m2[:, :, 0:32], in1=m2[:, :, 32:64], op=ALU.max)
+            mx = sb.tile([P, R], F32, name="mx", bufs=2)
+            nc.vector.tensor_reduce(out=mx[:], in_=m3[:], axis=AX.X, op=ALU.max)
+            nmx = sb.tile([P, R], F32, name="nmx", bufs=2)
+            nc.vector.tensor_scalar(out=nmx[:], in0=mx[:], scalar1=-1.0, scalar2=None, op0=ALU.mult)
+            ex = sb.tile([P, R, C], F32, name="ex", bufs=2, align_bytes=64)
+            tot = sb.tile([P, R], F32, name="tot", bufs=2)
+            for r in range(R):
+                nc.scalar.activation(out=ex[:, r, :], in_=l[:, r, :], func=ACT.Exp, bias=nmx[:, r:r + 1],
+                                     scale=1.0, accum_out=tot[:, r:r + 1])
+            e[b] = (ex, tot)
+
+        def assign(b):
+            ex, tot = e[b]
+            ri = sb.tile([P, R], F32, name="ri", bufs=2)
+            nc.vector.reciprocal(out=ri[:], in_=tot[:])
+            ar = sb.tile([P, R], F32, name="ar", bufs=2)
+            nc.vector.tensor_tensor(out=ar[:], in0=ri[:], in1=gr256[:], op=ALU.mult)
+            al = sb.tile([P, R], F32, name="al", bufs=2)
+            nc.vector.tensor_tensor(out=al[:], in0=ri[:], in1=gl8[:], op=ALU.mult)
+            srp = sb.tile([P, T, G, C], BF16, name="srp", bufs=2, align_bytes=64)
+            slp = sb.tile([P, T, G, C], BF16, name="slp", bufs=2, align_bytes=64)
+            for g in range(G):
+                for t in range(T):
+                    r = g * T + t
+                    nc.scalar.activation(out=srp[:, t, g, :], in_=ex[:, r, :], func=ACT.Identity,
+                                         bias=gr_n[:, r:r + 1], scale=ar[:, r:r + 1])
+            for g in range(G):
+                for t in range(T):
+                    r = g * T + t
+                    nc.scalar.activation(out=slp[:, t, g, :], in_=ex[:, r, :], func=ACT.Identity,
+                                         bias=gl_n[:, r:r + 1], scale=al[:, r:r + 1])
+            sri = sb.tile([P, G * C, T], BF16, name="sri", bufs=2, align_bytes=64)
+            interleave(sri, srp[:].rearrange("p t g c -> p t (g c)"), 2 if b == 0 else 1)
+            srq[b] = quant(sri[:].rearrange("p c t -> p (c t)"), G * C, "srq", 2)
+            sli = sb.tile([P, G * C, T], BF16, name="sli", bufs=2, align_bytes=64)
+            interleave(sli, slp[:].rearrange("p t g c -> p t (g c)"), 0)
+            slq[b] = quant(sli[:].rearrange("p c t -> p (c t)"), G * C, "slq", 2)
+
+        def interleave(dst, src, on_tensor):
+            flat = dst[:].rearrange("p c t -> p (c t)")
+            width = dst.shape[1]
+            for h in range(on_tensor):
+                il = ps.tile([P, 1024], BF16, name="il", tag="po", bufs=2)
+                for k in range(2):
+                    c0 = h * 256 + k * 128
+                    nc.tensor.matmul(il[:, k * 512:(k + 1) * 512], lhsT=ident_b[:],
+                                     rhs=src[:, :, c0:c0 + 128].rearrange("p t f -> p f t"), start=True, stop=True)
+                nc.scalar.copy(out=flat[:, h * 1024:(h + 1) * 1024], in_=il[:])
+            c0 = on_tensor * 256
+            if c0 < width:
+                nc.vector.tensor_copy(out=dst[:, c0:width, :].rearrange("p (c i) t -> p c t i", i=4),
+                                      in_=src[:, :, c0:width].rearrange("p t (c i) -> p c t i", i=4))
+
+        def quant(src, width, nm, bufs):
+            codes = sb.tile([P, width], U32, name=nm + "_c", bufs=bufs, align_bytes=64)
+            planes = sb.tile([P, width], U8, name=nm + "_s", bufs=bufs, align_bytes=64)
+            nc.vector.quantize_mx(out=codes[:].bitcast(FP8X4), scales=planes[:], in_=src)
+            return codes, planes
+
+        xq = {}
+
+        def prep_x(b, g):
+            xi = sb.tile([P, F, T], BF16, name="xi", bufs=2, align_bytes=64)
+            interleave(xi, xs[b, g][:], 2)
+            xq[b, g] = quant(xi[:].rearrange("p f t -> p (f t)"), F, "xq", 4)
+
+        sc = {}
+
+        def scale_adj(b, g):
+            for t in range(T):
+                s = sb.tile([P, N], BF16, name="adj_bf", bufs=8, align_bytes=64)
+                nc.vector.tensor_tensor(out=s[:], in0=raw[b, g][:, t, :].bitcast(FP8), in1=scale_sb[:], op=ALU.mult)
+                sc[b, g, t] = s
+
+        adjq = {}
+
+        def turn_adj(b, g, pair):
+            at = sb.tile([P, 2 * G * P * T], BF16, name="at", bufs=4, align_bytes=64)
+            words = at[:].bitcast(F32)
+            for ti in range(2):
+                src = sc[b, g, pair * 2 + ti][:].bitcast(F32)
+                tr = ps.tile([P, G, 2, P], F32, name="tr", bufs=2)
+                for gm in range(G):
+                    for u in range(2):
+                        nc.tensor.transpose(tr[:, gm, u, :], src[:, 256 * gm + u:256 * (gm + 1):2], ident_f[:])
+                nc.scalar.copy(out=words[:, ti * 512:(ti + 1) * 512].rearrange("p (g n u) -> p g n u", g=G, u=2),
+                               in_=tr[:].rearrange("p g u n -> p g n u"))
+            adjq[b, g, pair] = quant(at[:], 2 * G * P, "adjq", 4)
+
+        zf = {}
+        zq, qq = {}, {}
+
+        def mm(out, lhs, l0, rhs, r0, n, start, stop):
+            nc.tensor.matmul_mx(out=out, lhsT=lhs[0][:, l0:l0 + P].bitcast(FP8X4), lhsT_scale=lhs[1][:, l0:l0 + P],
+                                rhs=rhs[0][:, r0:r0 + n].bitcast(FP8X4), rhs_scale=rhs[1][:, r0:r0 + n],
+                                start=start, stop=stop)
+
+        def features(b, g, pair):
+            if pair == 0:
+                zf[b, g] = sb.tile([P, T, F], F32, name="zf", bufs=2, align_bytes=64)
+            for ti in range(2):
+                tp = ps.tile([P, F], F32, name="tp", bufs=2)
+                for gm in range(G):
+                    mm(tp[:], adjq[b, g, pair], ti * 256 + gm * P, xq[b, gm], 0, F, gm == 0, gm == G - 1)
+                nc.scalar.activation(out=zf[b, g][:, pair * 2 + ti, :], in_=tp[:], func=ACT.Gelu)
+
+        def go_view(g, n):
+            return go_f[:, g * T:(g + 1) * T].unsqueeze(1).unsqueeze(3).to_broadcast([P, n // 4, T, 4])
+
+        def gain_z(b, g):
+            zi = sb.tile([P, F, T], BF16, name="zi", bufs=2, align_bytes=64)
+            nc.vector.tensor_tensor(out=zi[:].rearrange("p (c i) t -> p c t i", i=4),
+                                    in0=zf[b, g][:].rearrange("p t (c i) -> p c t i", i=4),
+                                    in1=go_view(g, F), op=ALU.mult)
+            zq[b, g] = quant(zi[:].rearrange("p f t -> p (f t)"), F, "zq", 3)
+
+        def clusters(b, g):
+            qi = sb.tile([P, C, T], BF16, name="qi", bufs=2, align_bytes=64)
+            for h in range(2):
+                qp = ps.tile([P, T, P], F32, name="qp", bufs=2)
+                for t in range(T):
+                    for gm in range(G):
+                        mm(qp[:, t, :], adjq[b, g, t // 2], (t % 2) * 256 + gm * P, srq[b], gm * C + h * P, P,
+                           gm == 0, gm == G - 1)
+                nc.vector.tensor_tensor(out=qi[:, h * P:(h + 1) * P, :].rearrange("p (c i) t -> p c t i", i=4),
+                                        in0=qp[:].rearrange("p t (c i) -> p c t i", i=4),
+                                        in1=go_view(g, P), op=ALU.mult)
+            qq[b, g] = quant(qi[:].rearrange("p c t -> p (c t)"), C, "qq", 3)
+
+        def pool_x(b):
+            for ci in range(2):
+                po = ps.tile([P, F], F32, name="po_x", tag="po", bufs=2)
+                for g in range(G):
+                    mm(po[:], slq[b], g * C + ci * P, zq[b, g], 0, F, g == 0, g == G - 1)
+                o = sb.tile([P, F], F32, name="ox", bufs=2, align_bytes=64)
+                nc.scalar.copy(out=o[:], in_=po[:])
+                nc.sync.dma_start(out=out_0[b, ci * P:(ci + 1) * P, :], in_=o[:])
+
+        def pool_a(b):
+            for ci in range(2):
+                po = ps.tile([P, C], F32, name="po_a", tag="po", bufs=2)
+                for g in range(G):
+                    mm(po[:], slq[b], g * C + ci * P, qq[b, g], 0, C, g == 0, g == G - 1)
+                o = sb.tile([P, C], F32, name="oa", bufs=2, align_bytes=64)
+                if ci == 0:
+                    nc.scalar.copy(out=o[:], in_=po[:])
+                else:
+                    nc.vector.tensor_copy(out=o[:], in_=po[:])
+                nc.sync.dma_start(out=out_1[b, ci * P:(ci + 1) * P, :], in_=o[:])
+
+        softmax_exp(0)
+        scale_adj(0, 0)
+        softmax_exp(1)
+        turn_adj(0, 0, 0)
+        turn_adj(0, 0, 1)
+        prep_x(0, 0)
+        prep_x(0, 1)
+        scale_adj(0, 1)
+        features(0, 0, 0)
+        features(0, 0, 1)
+        assign(0)
+        turn_adj(0, 1, 0)
+        turn_adj(0, 1, 1)
+        gain_z(0, 0)
+        clusters(0, 0)
+        features(0, 1, 0)
+        features(0, 1, 1)
+        scale_adj(1, 0)
+        prep_x(1, 0)
+        prep_x(1, 1)
+        assign(1)
+        turn_adj(1, 0, 0)
+        turn_adj(1, 0, 1)
+        gain_z(0, 1)
+        clusters(0, 1)
+        features(1, 0, 0)
+        features(1, 0, 1)
+        pool_x(0)
+        pool_a(0)
+        scale_adj(1, 1)
+        turn_adj(1, 1, 0)
+        turn_adj(1, 1, 1)
+        gain_z(1, 0)
+        clusters(1, 0)
+        features(1, 1, 0)
+        features(1, 1, 1)
+        gain_z(1, 1)
+        clusters(1, 1)
+        pool_x(1)
+        pool_a(1)

@@ -8,6 +8,7 @@ P = 128
 T = 4
 G = N // (P * T)
 R = G * T
+MIX = 256
 
 F32 = mybir.dt.float32
 BF16 = mybir.dt.bfloat16
@@ -27,267 +28,466 @@ def tile_diffpoolcoarsen_kernel(tc, adj_bytes, adj_scale, logits, x, gr, gl, go,
     with ExitStack() as ctx:
         sb = ctx.enter_context(tc.tile_pool(name="sb", bufs=1))
         ps = ctx.enter_context(tc.psum_pool(name="ps", bufs=1))
+        ctx.enter_context(tc.manual_schedule())
 
         ident_f = sb.tile([P, P], F32, name="ident_f", align_bytes=64)
         make_identity(nc, ident_f[:])
         ident_b = sb.tile([P, P], BF16, name="ident_b", align_bytes=64)
         nc.gpsimd.tensor_copy(out=ident_b[:], in_=ident_f[:])
-        warm = sb.tile([P, 1], F32, name="warm")
-        nc.vector.memset(warm[:], 0.0)
-        warm2 = sb.tile([P, 1], F32, name="warm2")
-        nc.scalar.activation(out=warm2[:], in_=warm[:], func=ACT.Exp)
 
-        lg = []
-        raw = {}
-        xs = {}
+        zero = sb.tile([P, 1], F32, name="zero")
+        nc.vector.memset(zero[:], 0.0)
+        one = sb.tile([P, 1], F32, name="one")
+        nc.scalar.activation(out=one[:], in_=zero[:], func=ACT.Exp)
 
-        def load_logits(b):
-            t = sb.tile([P, G, T, C], BF16, name="lg", bufs=2, align_bytes=64)
-            nc.sync.dma_start(out=t[:], in_=logits[b].rearrange("(g p t) c -> p g t c", p=P, t=T))
-            lg.append(t)
+        scale_cols = sb.tile([P, 8], F32, name="scale_cols", align_bytes=64)
+        scale_row = sb.tile([P, N], F32, name="scale_row", align_bytes=64)
+        gain_r256, gain_r_neg, gain_l8, gain_l_neg, gain_o = [
+            sb.tile([P, R], F32, name=nm, align_bytes=64)
+            for nm in ("gain_r256", "gain_r_neg", "gain_l8", "gain_l_neg", "gain_o")
+        ]
 
-        def load_adj(b, g, split=1):
-            t = sb.tile([P, T, N], U8, name="adj_raw", bufs=4, align_bytes=64)
-            src = adj_bytes[b].rearrange("(g p t) m -> g p t m", p=P, t=T)[g]
-            w = T // split
-            for i in range(split):
-                nc.sync.dma_start(out=t[:, i * w:(i + 1) * w, :], in_=src[:, i * w:(i + 1) * w, :])
-            raw[b, g] = t
+        adj_raw, e, e_sum, right, left, mixed, maxima = {}, {}, {}, {}, {}, {}, {}
+        for b in range(B):
+            for g in range(G):
+                adj_raw[b, g] = sb.tile([P, T, N], U8, name="adj_raw", bufs=4, align_bytes=64)
+                mixed["x", b, g] = sb.tile([P, F, T], BF16, name="x_mixed", bufs=4, align_bytes=64)
+            e[b] = sb.tile([P, R, C], F32, name="e", bufs=2, align_bytes=64)
+            e_sum[b] = sb.tile([P, R], F32, name="e_sum", bufs=2)
+            right[b] = sb.tile([P, T, G, C], BF16, name="right", bufs=2, align_bytes=64)
+            left[b] = sb.tile([P, T, G, C], BF16, name="left", bufs=2, align_bytes=64)
+            mixed["r", b] = sb.tile([P, G * C, T], BF16, name="r_mixed", bufs=2, align_bytes=64)
+            mixed["l", b] = sb.tile([P, G * C, T], BF16, name="l_mixed", bufs=2, align_bytes=64)
+            for w in (128, 64, 32):
+                maxima[b, w] = sb.tile([P, R, w], BF16, name="max%d" % w, bufs=2, align_bytes=64)
+
+        lg, xs, gains = {}, {}, {}
+
+        def load_logits(b, g):
+            lg[b, g] = sb.tile([P, T, C], BF16, name="lg", bufs=4, align_bytes=64)
+            nc.sync.dma_start(out=lg[b, g][:], in_=logits[b].rearrange("(g p t) c -> g p t c", p=P, t=T)[g])
+
+        def load_adj(b, g, h):
+            rows = adj_bytes[b].rearrange("(g p t) m -> g p t m", p=P, t=T)[g]
+            nc.sync.dma_start(out=adj_raw[b, g][:, 2 * h:2 * h + 2, :], in_=rows[:, 2 * h:2 * h + 2, :])
 
         def load_x(b, g):
-            t = sb.tile([P, T, F], BF16, name="xs", bufs=4, align_bytes=64)
-            nc.sync.dma_start(out=t[:], in_=x[b].rearrange("(g p t) f -> g p t f", p=P, t=T)[g])
-            xs[b, g] = t
+            xs[b, g] = sb.tile([P, T, F], BF16, name="xs", bufs=4, align_bytes=64)
+            nc.sync.dma_start(out=xs[b, g][:], in_=x[b].rearrange("(g p t) f -> g p t f", p=P, t=T)[g])
 
-        gains = {}
-        for nm, src in (("gr", gr), ("gl", gl), ("go", go)):
-            t = sb.tile([P, G, T], BF16, name="gain_" + nm, align_bytes=64)
-            nc.gpsimd.dma_start(out=t[:], in_=src.rearrange("(g p t) -> p g t", p=P, t=T))
-            gains[nm] = t
+        def load_gain(nm):
+            vec = {"gr": gr, "gl": gl, "go": go}[nm]
+            gains[nm] = sb.tile([P, G, T], BF16, name="gain_" + nm, align_bytes=64)
+            nc.sync.dma_start(out=gains[nm][:], in_=vec.rearrange("(g p t) -> p g t", p=P, t=T))
 
-        load_logits(0)
-        scale_sb = sb.tile([P, N], F32, name="scale_sb", align_bytes=64)
-        nc.sync.dma_start(out=scale_sb[:], in_=adj_scale.rearrange("a b m -> (a b m)").partition_broadcast(P))
-        load_adj(0, 0, split=2)
-        load_logits(1)
-        load_x(0, 0)
-        load_x(0, 1)
-        load_adj(0, 1)
-        load_x(1, 0)
-        load_x(1, 1)
-        load_adj(1, 0)
-        load_adj(1, 1)
+        def load_scale():
+            nc.sync.dma_start(out=scale_cols[:], in_=adj_scale.rearrange("a b (n j) -> (a b n) j", j=8))
 
-        def gain_tile(nm, src, factor):
-            t = sb.tile([P, R], F32, name=nm, align_bytes=64)
-            nc.gpsimd.tensor_scalar(out=t[:], in0=gains[src][:].rearrange("p g t -> p (g t)"), scalar1=factor,
-                                    scalar2=0.0, op0=ALU.mult, op1=ALU.add)
-            return t
+        def widen_gain(nm):
+            uses = {
+                "gr": ((gain_r256, 256.0), (gain_r_neg, -1.0)),
+                "gl": ((gain_l8, 8.0), (gain_l_neg, -1.0 / 32.0)),
+                "go": ((gain_o, 1.0),),
+            }
+            for dst, factor in uses[nm]:
+                nc.gpsimd.tensor_scalar(out=dst[:], in0=gains[nm][:].rearrange("p g t -> p (g t)"), scalar1=factor,
+                                        scalar2=0.0, op0=ALU.mult, op1=ALU.add)
 
-        gr256 = gain_tile("gr256", "gr", 256.0)
-        gr_n = gain_tile("gr_n", "gr", -1.0)
-        gl8 = gain_tile("gl8", "gl", 8.0)
-        gl_n = gain_tile("gl_n", "gl", -1.0 / 32.0)
-        go_f = gain_tile("go_f", "go", 1.0)
+        spread = {}
 
-        e = {}
-        srq, slq = {}, {}
+        def spread_scale(h):
+            spread[h] = ps.tile([P, 4, P], F32, name="spread", tag="tr", bufs=2)
+            for j in range(4):
+                col = scale_cols[:, 4 * h + j:4 * h + j + 1]
+                nc.tensor.transpose(spread[h][:, j, :], col.to_broadcast([P, P]), ident_f[:])
 
-        def softmax_exp(b):
-            l = lg[b][:].rearrange("p g t c -> p (g t) c")
-            m1 = sb.tile([P, R, 128], BF16, name="m1", bufs=2, align_bytes=64)
-            nc.vector.tensor_tensor(out=m1[:], in0=l[:, :, 0:128], in1=l[:, :, 128:256], op=ALU.max)
-            m2 = sb.tile([P, R, 64], BF16, name="m2", bufs=2, align_bytes=64)
-            nc.vector.tensor_tensor(out=m2[:], in0=m1[:, :, 0:64], in1=m1[:, :, 64:128], op=ALU.max)
-            m3 = sb.tile([P, R, 32], BF16, name="m3", bufs=2, align_bytes=64)
-            nc.vector.tensor_tensor(out=m3[:], in0=m2[:, :, 0:32], in1=m2[:, :, 32:64], op=ALU.max)
-            mx = sb.tile([P, R], F32, name="mx", bufs=2)
-            nc.vector.tensor_reduce(out=mx[:], in_=m3[:], axis=AX.X, op=ALU.max)
-            nmx = sb.tile([P, R], F32, name="nmx", bufs=2)
-            nc.vector.tensor_scalar(out=nmx[:], in0=mx[:], scalar1=-1.0, scalar2=None, op0=ALU.mult)
-            ex = sb.tile([P, R, C], F32, name="ex", bufs=2, align_bytes=64)
-            tot = sb.tile([P, R], F32, name="tot", bufs=2)
-            for r in range(R):
-                nc.scalar.activation(out=ex[:, r, :], in_=l[:, r, :], func=ACT.Exp, bias=nmx[:, r:r + 1],
-                                     scale=1.0, accum_out=tot[:, r:r + 1])
-            e[b] = (ex, tot)
+        def gather_scale(h):
+            out = scale_row[:].rearrange("p (n j) -> p n j", j=8)[:, :, 4 * h:4 * h + 4]
+            src = spread[h][:].rearrange("p j n -> p n j")
+            if h == 0:
+                nc.scalar.copy(out=out, in_=src)
+            else:
+                nc.vector.tensor_copy(out=out, in_=src)
 
-        def assign(b):
-            ex, tot = e[b]
-            ri = sb.tile([P, R], F32, name="ri", bufs=2)
-            nc.vector.reciprocal(out=ri[:], in_=tot[:])
-            ar = sb.tile([P, R], F32, name="ar", bufs=2)
-            nc.vector.tensor_tensor(out=ar[:], in0=ri[:], in1=gr256[:], op=ALU.mult)
-            al = sb.tile([P, R], F32, name="al", bufs=2)
-            nc.vector.tensor_tensor(out=al[:], in0=ri[:], in1=gl8[:], op=ALU.mult)
-            srp = sb.tile([P, T, G, C], BF16, name="srp", bufs=2, align_bytes=64)
-            slp = sb.tile([P, T, G, C], BF16, name="slp", bufs=2, align_bytes=64)
-            for g in range(G):
-                for t in range(T):
-                    r = g * T + t
-                    nc.scalar.activation(out=srp[:, t, g, :], in_=ex[:, r, :], func=ACT.Identity,
-                                         bias=gr_n[:, r:r + 1], scale=ar[:, r:r + 1])
-            for g in range(G):
-                for t in range(T):
-                    r = g * T + t
-                    nc.scalar.activation(out=slp[:, t, g, :], in_=ex[:, r, :], func=ACT.Identity,
-                                         bias=gl_n[:, r:r + 1], scale=al[:, r:r + 1])
-            sri = sb.tile([P, G * C, T], BF16, name="sri", bufs=2, align_bytes=64)
-            interleave(sri, srp[:].rearrange("p t g c -> p t (g c)"), 2 if b == 0 else 1)
-            srq[b] = quant(sri[:].rearrange("p c t -> p (c t)"), G * C, "srq", 2)
-            sli = sb.tile([P, G * C, T], BF16, name="sli", bufs=2, align_bytes=64)
-            interleave(sli, slp[:].rearrange("p t g c -> p t (g c)"), 0)
-            slq[b] = quant(sli[:].rearrange("p c t -> p (c t)"), G * C, "slq", 2)
+        def max_first(b, g):
+            src = lg[b, g][:]
+            nc.vector.tensor_tensor(out=maxima[b, 128][:, g * T:(g + 1) * T, :], in0=src[:, :, 0:128],
+                                    in1=src[:, :, 128:256], op=ALU.max)
 
-        def interleave(dst, src, on_tensor):
-            flat = dst[:].rearrange("p c t -> p (c t)")
-            width = dst.shape[1]
-            for h in range(on_tensor):
-                il = ps.tile([P, 1024], BF16, name="il", tag="po", bufs=2)
-                for k in range(2):
-                    c0 = h * 256 + k * 128
-                    nc.tensor.matmul(il[:, k * 512:(k + 1) * 512], lhsT=ident_b[:],
-                                     rhs=src[:, :, c0:c0 + 128].rearrange("p t f -> p f t"), start=True, stop=True)
-                nc.scalar.copy(out=flat[:, h * 1024:(h + 1) * 1024], in_=il[:])
-            c0 = on_tensor * 256
-            if c0 < width:
-                nc.vector.tensor_copy(out=dst[:, c0:width, :].rearrange("p (c i) t -> p c t i", i=4),
-                                      in_=src[:, :, c0:width].rearrange("p t (c i) -> p c t i", i=4))
+        def max_half(b, w):
+            src = maxima[b, 2 * w][:]
+            nc.vector.tensor_tensor(out=maxima[b, w][:], in0=src[:, :, 0:w], in1=src[:, :, w:2 * w], op=ALU.max)
 
-        def quant(src, width, nm, bufs):
-            codes = sb.tile([P, width], U32, name=nm + "_c", bufs=bufs, align_bytes=64)
-            planes = sb.tile([P, width], U8, name=nm + "_s", bufs=bufs, align_bytes=64)
-            nc.vector.quantize_mx(out=codes[:].bitcast(FP8X4), scales=planes[:], in_=src)
-            return codes, planes
+        neg_max = {}
 
-        xq = {}
+        def max_last(b):
+            neg_max[b] = sb.tile([P, R], F32, name="neg_max", bufs=2)
+            nc.vector.tensor_reduce(out=neg_max[b][:], in_=maxima[b, 32][:], axis=AX.X, op=ALU.max, negate=True)
 
-        def prep_x(b, g):
-            xi = sb.tile([P, F, T], BF16, name="xi", bufs=2, align_bytes=64)
-            interleave(xi, xs[b, g][:], 2)
-            xq[b, g] = quant(xi[:].rearrange("p f t -> p (f t)"), F, "xq", 4)
-
-        sc = {}
-
-        def scale_adj(b, g):
+        def exps(b, g):
             for t in range(T):
-                s = sb.tile([P, N], BF16, name="adj_bf", bufs=8, align_bytes=64)
-                nc.vector.tensor_tensor(out=s[:], in0=raw[b, g][:, t, :].bitcast(FP8), in1=scale_sb[:], op=ALU.mult)
-                sc[b, g, t] = s
+                r = g * T + t
+                nc.scalar.activation(out=e[b][:, r, :], in_=lg[b, g][:, t, :], func=ACT.Exp,
+                                     bias=neg_max[b][:, r:r + 1], scale=1.0, accum_out=e_sum[b][:, r:r + 1])
 
-        adjq = {}
+        inverse, slope_r, slope_l = {}, {}, {}
 
-        def turn_adj(b, g, pair):
-            at = sb.tile([P, 2 * G * P * T], BF16, name="at", bufs=4, align_bytes=64)
-            words = at[:].bitcast(F32)
-            for ti in range(2):
-                src = sc[b, g, pair * 2 + ti][:].bitcast(F32)
-                tr = ps.tile([P, G, 2, P], F32, name="tr", bufs=2)
-                for gm in range(G):
-                    for u in range(2):
-                        nc.tensor.transpose(tr[:, gm, u, :], src[:, 256 * gm + u:256 * (gm + 1):2], ident_f[:])
-                nc.scalar.copy(out=words[:, ti * 512:(ti + 1) * 512].rearrange("p (g n u) -> p g n u", g=G, u=2),
-                               in_=tr[:].rearrange("p g u n -> p g n u"))
-            adjq[b, g, pair] = quant(at[:], 2 * G * P, "adjq", 4)
+        def invert(b):
+            inverse[b] = sb.tile([P, R], F32, name="inverse", bufs=2)
+            nc.vector.reciprocal(out=inverse[b][:], in_=e_sum[b][:])
 
-        zf = {}
-        zq, qq = {}, {}
+        def slopes(b):
+            slope_r[b] = sb.tile([P, R], F32, name="slope_r", bufs=2)
+            nc.gpsimd.tensor_tensor(out=slope_r[b][:], in0=inverse[b][:], in1=gain_r256[:], op=ALU.mult)
+            slope_l[b] = sb.tile([P, R], F32, name="slope_l", bufs=2)
+            nc.gpsimd.tensor_tensor(out=slope_l[b][:], in0=inverse[b][:], in1=gain_l8[:], op=ALU.mult)
 
-        def mm(out, lhs, l0, rhs, r0, n, start, stop):
-            nc.tensor.matmul_mx(out=out, lhsT=lhs[0][:, l0:l0 + P].bitcast(FP8X4), lhsT_scale=lhs[1][:, l0:l0 + P],
-                                rhs=rhs[0][:, r0:r0 + n].bitcast(FP8X4), rhs_scale=rhs[1][:, r0:r0 + n],
-                                start=start, stop=stop)
-
-        def features(b, g, pair):
-            if pair == 0:
-                zf[b, g] = sb.tile([P, T, F], F32, name="zf", bufs=2, align_bytes=64)
-            for ti in range(2):
-                tp = ps.tile([P, F], F32, name="tp", bufs=2)
-                for gm in range(G):
-                    mm(tp[:], adjq[b, g, pair], ti * 256 + gm * P, xq[b, gm], 0, F, gm == 0, gm == G - 1)
-                nc.scalar.activation(out=zf[b, g][:, pair * 2 + ti, :], in_=tp[:], func=ACT.Gelu)
-
-        def go_view(g, n):
-            return go_f[:, g * T:(g + 1) * T].unsqueeze(1).unsqueeze(3).to_broadcast([P, n // 4, T, 4])
-
-        def gain_z(b, g):
-            zi = sb.tile([P, F, T], BF16, name="zi", bufs=2, align_bytes=64)
-            nc.vector.tensor_tensor(out=zi[:].rearrange("p (c i) t -> p c t i", i=4),
-                                    in0=zf[b, g][:].rearrange("p t (c i) -> p c t i", i=4),
-                                    in1=go_view(g, F), op=ALU.mult)
-            zq[b, g] = quant(zi[:].rearrange("p f t -> p (f t)"), F, "zq", 3)
-
-        def clusters(b, g):
-            qi = sb.tile([P, C, T], BF16, name="qi", bufs=2, align_bytes=64)
-            for h in range(2):
-                qp = ps.tile([P, T, P], F32, name="qp", bufs=2)
-                for t in range(T):
-                    for gm in range(G):
-                        mm(qp[:, t, :], adjq[b, g, t // 2], (t % 2) * 256 + gm * P, srq[b], gm * C + h * P, P,
-                           gm == 0, gm == G - 1)
-                nc.vector.tensor_tensor(out=qi[:, h * P:(h + 1) * P, :].rearrange("p (c i) t -> p c t i", i=4),
-                                        in0=qp[:].rearrange("p t (c i) -> p c t i", i=4),
-                                        in1=go_view(g, P), op=ALU.mult)
-            qq[b, g] = quant(qi[:].rearrange("p c t -> p (c t)"), C, "qq", 3)
-
-        def pool_x(b):
-            for ci in range(2):
-                po = ps.tile([P, F], F32, name="po_x", tag="po", bufs=2)
-                for g in range(G):
-                    mm(po[:], slq[b], g * C + ci * P, zq[b, g], 0, F, g == 0, g == G - 1)
-                o = sb.tile([P, F], F32, name="ox", bufs=2, align_bytes=64)
-                nc.scalar.copy(out=o[:], in_=po[:])
-                nc.sync.dma_start(out=out_0[b, ci * P:(ci + 1) * P, :], in_=o[:])
-
-        def pool_a(b):
-            for ci in range(2):
-                po = ps.tile([P, C], F32, name="po_a", tag="po", bufs=2)
-                for g in range(G):
-                    mm(po[:], slq[b], g * C + ci * P, qq[b, g], 0, C, g == 0, g == G - 1)
-                o = sb.tile([P, C], F32, name="oa", bufs=2, align_bytes=64)
-                if ci == 0:
-                    nc.scalar.copy(out=o[:], in_=po[:])
+        def assign(engine, name, b, g, slots):
+            dst, slope, shift = {"r": (right, slope_r, gain_r_neg), "l": (left, slope_l, gain_l_neg)}[name]
+            for t in slots:
+                r = g * T + t
+                factor, offset = slope[b][:, r:r + 1], shift[:, r:r + 1]
+                if engine == "scalar":
+                    nc.scalar.activation(out=dst[b][:, t, g, :], in_=e[b][:, r, :], func=ACT.Identity,
+                                         bias=offset, scale=factor)
                 else:
-                    nc.vector.tensor_copy(out=o[:], in_=po[:])
-                nc.sync.dma_start(out=out_1[b, ci * P:(ci + 1) * P, :], in_=o[:])
+                    nc.vector.tensor_scalar(out=dst[b][:, t, g, :], in0=e[b][:, r, :], scalar1=factor,
+                                            scalar2=offset, op0=ALU.mult, op1=ALU.add)
 
-        softmax_exp(0)
-        scale_adj(0, 0)
-        softmax_exp(1)
-        turn_adj(0, 0, 0)
-        turn_adj(0, 0, 1)
-        prep_x(0, 0)
-        prep_x(0, 1)
-        scale_adj(0, 1)
-        features(0, 0, 0)
-        features(0, 0, 1)
-        assign(0)
-        turn_adj(0, 1, 0)
-        turn_adj(0, 1, 1)
-        gain_z(0, 0)
+        def slot_rows(key, h):
+            if key[0] == "x":
+                rows = xs[key[1], key[2]][:]
+            else:
+                rows = {"r": right, "l": left}[key[0]][key[1]][:].rearrange("p t g c -> p t (g c)")
+            return rows[:, :, h * MIX:(h + 1) * MIX]
+
+        banks = {}
+
+        def mix_tensor(key, h):
+            rows = slot_rows(key, h)
+            banks[key, h] = ps.tile([P, MIX * T], BF16, name="bank", tag="po", bufs=2)
+            for i in range(2):
+                half = rows[:, :, i * 128:(i + 1) * 128]
+                nc.tensor.matmul(banks[key, h][:, i * 512:(i + 1) * 512], lhsT=ident_b[:],
+                                 rhs=half.rearrange("p t c -> p c t"), start=True, stop=True)
+
+        def mix_out(key, h):
+            nc.scalar.copy(out=mixed[key][:, h * MIX:(h + 1) * MIX, :].rearrange("p c t -> p (c t)"), in_=banks[key, h][:])
+
+        def mix(engine, key, h):
+            dst = mixed[key][:, h * MIX:(h + 1) * MIX, :]
+            rows = slot_rows(key, h)
+            if engine == "tensor":
+                mix_tensor(key, h)
+                mix_out(key, h)
+            elif engine == "scalar":
+                nc.scalar.copy(out=dst, in_=rows.rearrange("p t c -> p c t"))
+            else:
+                nc.vector.tensor_copy(out=dst.rearrange("p (c i) t -> p c t i", i=4),
+                                      in_=rows.rearrange("p t (c i) -> p c t i", i=4))
+
+        def quantise(src, width, nm, bufs):
+            codes = sb.tile([P, width], U32, name=nm + "_codes", bufs=bufs, align_bytes=64)
+            scales = sb.tile([P, width], U8, name=nm + "_scales", bufs=bufs, align_bytes=64)
+            nc.vector.quantize_mx(out=codes[:].bitcast(FP8X4), scales=scales[:], in_=src)
+            return codes, scales
+
+        xq, rq, lq, zq, qq, adjq = {}, {}, {}, {}, {}, {}
+
+        def quant_x(b, g):
+            xq[b, g] = quantise(mixed["x", b, g][:].rearrange("p f t -> p (f t)"), F, "xq", 4)
+
+        def quant_r(b):
+            rq[b] = quantise(mixed["r", b][:].rearrange("p c t -> p (c t)"), G * C, "rq", 2)
+
+        def quant_l(b):
+            lq[b] = quantise(mixed["l", b][:].rearrange("p c t -> p (c t)"), G * C, "lq", 2)
+
+        adj_bf, adj_t, turned = {}, {}, {}
+
+        def scale_adj(i):
+            adj_bf[i] = sb.tile([P, N], BF16, name="adj_bf", bufs=6, align_bytes=64)
+            nc.vector.tensor_tensor(out=adj_bf[i][:], in0=adj_raw[i // R, i // T % G][:, i % T, :].bitcast(FP8),
+                                    in1=scale_row[:], op=ALU.mult)
+
+        def turn_tensor(i):
+            words = adj_bf[i][:].bitcast(F32)
+            turned[i] = ps.tile([P, G, 2, P], F32, name="turned", tag="tr", bufs=2)
+            for g in range(G):
+                for u in range(2):
+                    nc.tensor.transpose(turned[i][:, g, u, :], words[:, 256 * g + u:256 * (g + 1):2], ident_f[:])
+
+        def turn_out(i):
+            if i // 2 not in adj_t:
+                adj_t[i // 2] = sb.tile([P, 2 * G * P * T], BF16, name="adj_t", bufs=3, align_bytes=64)
+            words = adj_t[i // 2][:].bitcast(F32)[:, i % 2 * 512:(i % 2 + 1) * 512]
+            nc.scalar.copy(out=words.rearrange("p (g n u) -> p g n u", g=G, u=2),
+                           in_=turned[i][:].rearrange("p g u n -> p g n u"))
+
+        def turn(i):
+            turn_tensor(i)
+            turn_out(i)
+
+        def quant_adj(j):
+            adjq[j] = quantise(adj_t[j][:], 2 * G * P, "adjq", 4)
+
+        def product(out, lhs, l0, rhs, r0, width, g):
+            nc.tensor.matmul_mx(out=out, lhsT=lhs[0][:, l0:l0 + P].bitcast(FP8X4), lhsT_scale=lhs[1][:, l0:l0 + P],
+                                rhs=rhs[0][:, r0:r0 + width].bitcast(FP8X4), rhs_scale=rhs[1][:, r0:r0 + width],
+                                start=g == 0, stop=g == G - 1)
+
+        sums, gelus, z_mixed, q_sums, q_mixed = {}, {}, {}, {}, {}
+
+        def feat_tensor(i):
+            sums[i] = ps.tile([P, F], F32, name="sums", bufs=2)
+            for g in range(G):
+                product(sums[i][:], adjq[i // 2], i % 2 * 256 + g * P, xq[i // R, g], 0, F, g)
+
+        def feat_out(i):
+            if i // T not in gelus:
+                gelus[i // T] = sb.tile([P, T, F], F32, name="gelus", bufs=2, align_bytes=64)
+            nc.scalar.activation(out=gelus[i // T][:, i % T, :], in_=sums[i][:], func=ACT.Gelu)
+
+        def feat(i):
+            feat_tensor(i)
+            feat_out(i)
+
+        def gain_z(u):
+            z_mixed[u] = sb.tile([P, F, T], BF16, name="z_mixed", bufs=2, align_bytes=64)
+            gain = gain_o[:, u % G * T:(u % G + 1) * T].unsqueeze(1).unsqueeze(3)
+            nc.vector.tensor_tensor(out=z_mixed[u][:].rearrange("p (f i) t -> p f t i", i=4),
+                                    in0=gelus[u][:].rearrange("p t (f i) -> p f t i", i=4),
+                                    in1=gain.to_broadcast([P, F // 4, T, 4]), op=ALU.mult)
+
+        def quant_z(u):
+            zq[u // G, u % G] = quantise(z_mixed[u][:].rearrange("p f t -> p (f t)"), F, "zq", 3)
+
+        def clusters(u, h):
+            q_sums[u, h] = ps.tile([P, T, P], F32, name="q_sums", bufs=2)
+            for t in range(T):
+                for g in range(G):
+                    product(q_sums[u, h][:, t, :], adjq[2 * u + t // 2], t % 2 * 256 + g * P, rq[u // G], g * C + h * P, P, g)
+
+        def gain_q(u, h):
+            if u not in q_mixed:
+                q_mixed[u] = sb.tile([P, C, T], BF16, name="q_mixed", bufs=2, align_bytes=64)
+            gain = gain_o[:, u % G * T:(u % G + 1) * T].unsqueeze(1)
+            nc.vector.tensor_tensor(out=q_mixed[u][:, h * P:(h + 1) * P, :], in0=q_sums[u, h][:].rearrange("p t c -> p c t"),
+                                    in1=gain.to_broadcast([P, P, T]), op=ALU.mult)
+
+        def quant_q(u):
+            qq[u // G, u % G] = quantise(q_mixed[u][:].rearrange("p c t -> p (c t)"), C, "qq", 3)
+
+        def pool(engine, name, b, h):
+            width, rhs, out = {"x": (F, zq, out_0), "a": (C, qq, out_1)}[name]
+            pooled = ps.tile([P, width], F32, name="pooled_" + name, tag="po", bufs=2)
+            for g in range(G):
+                product(pooled[:], lq[b], g * C + h * P, rhs[b, g], 0, width, g)
+            result = sb.tile([P, width], F32, name="result_" + name, bufs=2, align_bytes=64)
+            if engine == "scalar":
+                nc.scalar.copy(out=result[:], in_=pooled[:])
+            else:
+                nc.vector.tensor_copy(out=result[:], in_=pooled[:])
+            nc.sync.dma_start(out=out[b, h * P:(h + 1) * P, :], in_=result[:])
+
+        load_logits(0, 1)
+        load_scale()
+        load_logits(0, 0)
+        spread_scale(1)
+        spread_scale(0)
+        max_first(0, 1)
+        max_first(0, 0)
+        max_half(0, 64)
+        load_logits(1, 1)
+        max_first(1, 1)
+        load_logits(1, 0)
+        gather_scale(1)
+        load_adj(0, 0, 0)
+        load_gain("gr")
+        max_half(0, 32)
+        max_first(1, 0)
+        gather_scale(0)
+        max_last(0)
+        max_half(1, 64)
+        scale_adj(0)
+        max_half(1, 32)
+        load_adj(0, 0, 1)
+        load_x(0, 1)
+        scale_adj(2)
+        exps(0, 0)
+        load_gain("gl")
+        max_last(1)
+        exps(0, 1)
+        scale_adj(1)
+        widen_gain("gr")
+        exps(1, 0)
+        scale_adj(3)
+        invert(0)
+        widen_gain("gl")
+        slopes(0)
+        exps(1, 1)
+        turn(0)
+        load_adj(0, 1, 0)
+        scale_adj(5)
+        assign("scalar", "l", 0, 1, (3,))
+        assign("vector", "r", 0, 1, (2,))
+        invert(1)
+        load_adj(0, 1, 1)
+        assign("vector", "l", 0, 1, (0,))
+        load_x(0, 0)
+        load_adj(1, 0, 0)
+        scale_adj(4)
+        assign("scalar", "r", 0, 1, (1,))
+        mix("tensor", ("x", 0, 1), 0)
+        turn(2)
+        assign("scalar", "r", 0, 1, (0,))
+        load_gain("go")
+        assign("scalar", "l", 0, 1, (1,))
+        mix("tensor", ("x", 0, 1), 1)
+        scale_adj(6)
+        assign("vector", "r", 0, 0, (1,))
+        scale_adj(7)
+        assign("scalar", "r", 0, 0, (0,))
+        turn(3)
+        mix_tensor(("x", 0, 0), 1)
+        assign("vector", "r", 0, 0, (3,))
+        slopes(1)
+        assign("scalar", "r", 0, 1, (3,))
+        turn(1)
+        quant_adj(1)
+        quant_x(0, 1)
+        mix_out(("x", 0, 0), 1)
+        load_x(1, 0)
+        assign("scalar", "r", 0, 0, (2,))
+        mix("tensor", ("x", 0, 0), 0)
+        turn(4)
+        quant_adj(0)
+        load_adj(1, 0, 1)
+        turn(5)
+        mix("vector", ("r", 0), 1)
+        widen_gain("go")
+        quant_x(0, 0)
+        scale_adj(8)
+        assign("vector", "l", 0, 0, (3,))
+        quant_adj(2)
+        load_adj(1, 1, 0)
+        load_adj(1, 1, 1)
+        assign("scalar", "r", 1, 1, (0,))
+        assign("scalar", "l", 0, 0, (1,))
+        mix("tensor", ("r", 0), 0)
+        assign("scalar", "r", 1, 1, (3,))
+        turn(6)
+        turn(7)
+        scale_adj(10)
+        feat(0)
+        quant_r(0)
+        scale_adj(9)
+        feat(3)
+        mix_tensor(("x", 1, 0), 1)
+        turn_tensor(8)
+        load_x(1, 1)
+        assign("scalar", "r", 1, 1, (2,))
+        scale_adj(11)
+        turn_tensor(10)
         clusters(0, 0)
-        features(0, 1, 0)
-        features(0, 1, 1)
-        scale_adj(1, 0)
-        prep_x(1, 0)
-        prep_x(1, 1)
-        assign(1)
-        turn_adj(1, 0, 0)
-        turn_adj(1, 0, 1)
-        gain_z(0, 1)
-        clusters(0, 1)
-        features(1, 0, 0)
-        features(1, 0, 1)
-        pool_x(0)
-        pool_a(0)
-        scale_adj(1, 1)
-        turn_adj(1, 1, 0)
-        turn_adj(1, 1, 1)
-        gain_z(1, 0)
+        quant_adj(3)
+        assign("scalar", "l", 0, 0, (2,))
+        mix("scalar", ("x", 1, 0), 0)
+        feat(1)
+        assign("scalar", "l", 0, 1, (2,))
         clusters(1, 0)
-        features(1, 1, 0)
-        features(1, 1, 1)
-        gain_z(1, 1)
+        scale_adj(13)
+        mix("vector", ("x", 1, 1), 1)
+        gain_q(0, 0)
+        mix("scalar", ("x", 1, 1), 0)
+        feat(2)
+        gain_q(1, 0)
+        assign("vector", "l", 1, 0, (3,))
+        scale_adj(12)
+        assign("scalar", "r", 1, 0, (1,))
+        turn_out(8)
+        assign("scalar", "r", 1, 0, (2,))
+        turn_out(10)
+        feat(4)
         clusters(1, 1)
-        pool_x(1)
-        pool_a(1)
+        clusters(0, 1)
+        feat_tensor(5)
+        quant_x(1, 1)
+        turn(11)
+        gain_q(1, 1)
+        gain_z(0)
+        assign("vector", "r", 1, 0, (0,))
+        gain_q(0, 1)
+        scale_adj(14)
+        feat_out(5)
+        mix_out(("x", 1, 0), 1)
+        quant_adj(5)
+        assign("scalar", "r", 1, 1, (1,))
+        assign("scalar", "r", 1, 0, (3,))
+        turn(9)
+        mix_tensor(("l", 0), 1)
+        assign("scalar", "l", 0, 0, (0,))
+        feat(6)
+        quant_x(1, 0)
+        mix("scalar", ("r", 1), 1)
+        feat(7)
+        quant_adj(4)
+        scale_adj(15)
+        quant_z(0)
+        mix_out(("l", 0), 1)
+        turn(12)
+        turn(14)
+        gain_z(1)
+        mix_tensor(("r", 1), 0)
+        feat(8)
+        mix_out(("r", 1), 0)
+        feat(10)
+        turn(13)
+        mix("vector", ("l", 0), 0)
+        turn_tensor(15)
+        quant_r(1)
+        assign("vector", "l", 1, 0, (2,))
+        quant_z(1)
+        quant_q(0)
+        quant_adj(6)
+        quant_q(1)
+        assign("scalar", "l", 1, 1, (2,))
+        feat(9)
+        turn_out(15)
+        feat(11)
+        clusters(2, 0)
+        quant_adj(7)
+        quant_l(0)
+        assign("scalar", "l", 1, 1, (0,))
+        assign("scalar", "l", 1, 0, (0,))
+        feat(12)
+        assign("scalar", "l", 1, 1, (3,))
+        feat(13)
+        gain_z(2)
+        gain_q(2, 0)
+        assign("scalar", "l", 1, 0, (1,))
+        pool("scalar", "x", 0, 0)
+        feat(14)
+        feat(15)
+        quant_z(2)
+        assign("scalar", "l", 1, 1, (1,))
+        pool("scalar", "x", 0, 1)
+        clusters(3, 0)
+        gain_z(3)
+        gain_q(3, 0)
+        mix("scalar", ("l", 1), 1)
+        mix("tensor", ("l", 1), 0)
+        clusters(2, 1)
+        pool("scalar", "a", 0, 1)
+        quant_l(1)
+        pool("scalar", "a", 0, 0)
+        clusters(3, 1)
+        quant_z(3)
+        pool("scalar", "x", 1, 0)
+        pool("scalar", "x", 1, 1)
+        gain_q(2, 1)
+        gain_q(3, 1)
+        quant_q(2)
+        quant_q(3)
+        pool("vector", "a", 1, 1)
+        pool("vector", "a", 1, 0)

from contextlib import ExitStack

import concourse.mybir as mybir
from concourse.masks import make_identity

B, N, F, C = 2, 1024, 512, 256
P = 128
T = 4
G = N // (P * T)
R = G * T
MIX = 256

F32 = mybir.dt.float32
BF16 = mybir.dt.bfloat16
U32 = mybir.dt.uint32
U8 = mybir.dt.uint8
FP8 = mybir.dt.float8_e4m3fn
FP8X4 = mybir.dt.float8_e4m3fn_x4
ALU = mybir.AluOpType
ACT = mybir.ActivationFunctionType
AX = mybir.AxisListType

FLOPS = 2 * B * (N * N * (F + C) + C * N * (F + C))


def tile_diffpoolcoarsen_kernel(tc, adj_bytes, adj_scale, logits, x, gr, gl, go, out_0, out_1):
    nc = tc.nc
    with ExitStack() as ctx:
        sb = ctx.enter_context(tc.tile_pool(name="sb", bufs=1))
        ps = ctx.enter_context(tc.psum_pool(name="ps", bufs=1))
        ctx.enter_context(tc.manual_schedule())

        ident_f = sb.tile([P, P], F32, name="ident_f", align_bytes=64)
        make_identity(nc, ident_f[:])
        ident_b = sb.tile([P, P], BF16, name="ident_b", align_bytes=64)
        nc.gpsimd.tensor_copy(out=ident_b[:], in_=ident_f[:])

        zero = sb.tile([P, 1], F32, name="zero")
        nc.vector.memset(zero[:], 0.0)
        one = sb.tile([P, 1], F32, name="one")
        nc.scalar.activation(out=one[:], in_=zero[:], func=ACT.Exp)

        scale_cols = sb.tile([P, 8], F32, name="scale_cols", align_bytes=64)
        scale_row = sb.tile([P, N], F32, name="scale_row", align_bytes=64)
        gain_r256, gain_r_neg, gain_l8, gain_l_neg, gain_o = [
            sb.tile([P, R], F32, name=nm, align_bytes=64)
            for nm in ("gain_r256", "gain_r_neg", "gain_l8", "gain_l_neg", "gain_o")
        ]

        adj_raw, e, e_sum, right, left, mixed, maxima = {}, {}, {}, {}, {}, {}, {}
        for b in range(B):
            for g in range(G):
                adj_raw[b, g] = sb.tile([P, T, N], U8, name="adj_raw", bufs=4, align_bytes=64)
                mixed["x", b, g] = sb.tile([P, F, T], BF16, name="x_mixed", bufs=4, align_bytes=64)
            e[b] = sb.tile([P, R, C], F32, name="e", bufs=2, align_bytes=64)
            e_sum[b] = sb.tile([P, R], F32, name="e_sum", bufs=2)
            right[b] = sb.tile([P, T, G, C], BF16, name="right", bufs=2, align_bytes=64)
            left[b] = sb.tile([P, T, G, C], BF16, name="left", bufs=2, align_bytes=64)
            mixed["r", b] = sb.tile([P, G * C, T], BF16, name="r_mixed", bufs=2, align_bytes=64)
            mixed["l", b] = sb.tile([P, G * C, T], BF16, name="l_mixed", bufs=2, align_bytes=64)
            for w in (128, 64, 32):
                maxima[b, w] = sb.tile([P, R, w], BF16, name="max%d" % w, bufs=2, align_bytes=64)

        lg, xs, gains = {}, {}, {}

        def load_logits(b, g):
            lg[b, g] = sb.tile([P, T, C], BF16, name="lg", bufs=4, align_bytes=64)
            nc.sync.dma_start(out=lg[b, g][:], in_=logits[b].rearrange("(g p t) c -> g p t c", p=P, t=T)[g])

        def load_adj(b, g, h):
            rows = adj_bytes[b].rearrange("(g p t) m -> g p t m", p=P, t=T)[g]
            nc.sync.dma_start(out=adj_raw[b, g][:, 2 * h:2 * h + 2, :], in_=rows[:, 2 * h:2 * h + 2, :])

        def load_x(b, g):
            xs[b, g] = sb.tile([P, T, F], BF16, name="xs", bufs=4, align_bytes=64)
            nc.sync.dma_start(out=xs[b, g][:], in_=x[b].rearrange("(g p t) f -> g p t f", p=P, t=T)[g])

        def load_gain(nm):
            vec = {"gr": gr, "gl": gl, "go": go}[nm]
            gains[nm] = sb.tile([P, G, T], BF16, name="gain_" + nm, align_bytes=64)
            nc.sync.dma_start(out=gains[nm][:], in_=vec.rearrange("(g p t) -> p g t", p=P, t=T))

        def load_scale():
            nc.sync.dma_start(out=scale_cols[:], in_=adj_scale.rearrange("a b (n j) -> (a b n) j", j=8))

        def widen_gain(nm):
            uses = {
                "gr": ((gain_r256, 256.0), (gain_r_neg, -1.0)),
                "gl": ((gain_l8, 8.0), (gain_l_neg, -1.0 / 32.0)),
                "go": ((gain_o, 1.0),),
            }
            for dst, factor in uses[nm]:
                nc.gpsimd.tensor_scalar(out=dst[:], in0=gains[nm][:].rearrange("p g t -> p (g t)"), scalar1=factor,
                                        scalar2=0.0, op0=ALU.mult, op1=ALU.add)

        spread = {}

        def spread_scale(h):
            spread[h] = ps.tile([P, 4, P], F32, name="spread", tag="tr", bufs=2)
            for j in range(4):
                col = scale_cols[:, 4 * h + j:4 * h + j + 1]
                nc.tensor.transpose(spread[h][:, j, :], col.to_broadcast([P, P]), ident_f[:])

        def gather_scale(h):
            out = scale_row[:].rearrange("p (n j) -> p n j", j=8)[:, :, 4 * h:4 * h + 4]
            src = spread[h][:].rearrange("p j n -> p n j")
            if h == 0:
                nc.scalar.copy(out=out, in_=src)
            else:
                nc.vector.tensor_copy(out=out, in_=src)

        def max_first(b, g):
            src = lg[b, g][:]
            nc.vector.tensor_tensor(out=maxima[b, 128][:, g * T:(g + 1) * T, :], in0=src[:, :, 0:128],
                                    in1=src[:, :, 128:256], op=ALU.max)

        def max_half(b, w):
            src = maxima[b, 2 * w][:]
            nc.vector.tensor_tensor(out=maxima[b, w][:], in0=src[:, :, 0:w], in1=src[:, :, w:2 * w], op=ALU.max)

        neg_max = {}

        def max_last(b):
            neg_max[b] = sb.tile([P, R], F32, name="neg_max", bufs=2)
            nc.vector.tensor_reduce(out=neg_max[b][:], in_=maxima[b, 32][:], axis=AX.X, op=ALU.max, negate=True)

        def exps(b, g):
            for t in range(T):
                r = g * T + t
                nc.scalar.activation(out=e[b][:, r, :], in_=lg[b, g][:, t, :], func=ACT.Exp,
                                     bias=neg_max[b][:, r:r + 1], scale=1.0, accum_out=e_sum[b][:, r:r + 1])

        inverse, slope_r, slope_l = {}, {}, {}

        def invert(b):
            inverse[b] = sb.tile([P, R], F32, name="inverse", bufs=2)
            nc.vector.reciprocal(out=inverse[b][:], in_=e_sum[b][:])

        def slopes(b):
            slope_r[b] = sb.tile([P, R], F32, name="slope_r", bufs=2)
            nc.gpsimd.tensor_tensor(out=slope_r[b][:], in0=inverse[b][:], in1=gain_r256[:], op=ALU.mult)
            slope_l[b] = sb.tile([P, R], F32, name="slope_l", bufs=2)
            nc.gpsimd.tensor_tensor(out=slope_l[b][:], in0=inverse[b][:], in1=gain_l8[:], op=ALU.mult)

        def assign(engine, name, b, g, slots):
            dst, slope, shift = {"r": (right, slope_r, gain_r_neg), "l": (left, slope_l, gain_l_neg)}[name]
            for t in slots:
                r = g * T + t
                factor, offset = slope[b][:, r:r + 1], shift[:, r:r + 1]
                if engine == "scalar":
                    nc.scalar.activation(out=dst[b][:, t, g, :], in_=e[b][:, r, :], func=ACT.Identity,
                                         bias=offset, scale=factor)
                else:
                    nc.vector.tensor_scalar(out=dst[b][:, t, g, :], in0=e[b][:, r, :], scalar1=factor,
                                            scalar2=offset, op0=ALU.mult, op1=ALU.add)

        def slot_rows(key, h):
            if key[0] == "x":
                rows = xs[key[1], key[2]][:]
            else:
                rows = {"r": right, "l": left}[key[0]][key[1]][:].rearrange("p t g c -> p t (g c)")
            return rows[:, :, h * MIX:(h + 1) * MIX]

        banks = {}

        def mix_tensor(key, h):
            rows = slot_rows(key, h)
            banks[key, h] = ps.tile([P, MIX * T], BF16, name="bank", tag="po", bufs=2)
            for i in range(2):
                half = rows[:, :, i * 128:(i + 1) * 128]
                nc.tensor.matmul(banks[key, h][:, i * 512:(i + 1) * 512], lhsT=ident_b[:],
                                 rhs=half.rearrange("p t c -> p c t"), start=True, stop=True)

        def mix_out(key, h):
            nc.scalar.copy(out=mixed[key][:, h * MIX:(h + 1) * MIX, :].rearrange("p c t -> p (c t)"), in_=banks[key, h][:])

        def mix(engine, key, h):
            dst = mixed[key][:, h * MIX:(h + 1) * MIX, :]
            rows = slot_rows(key, h)
            if engine == "tensor":
                mix_tensor(key, h)
                mix_out(key, h)
            elif engine == "scalar":
                nc.scalar.copy(out=dst, in_=rows.rearrange("p t c -> p c t"))
            else:
                nc.vector.tensor_copy(out=dst.rearrange("p (c i) t -> p c t i", i=4),
                                      in_=rows.rearrange("p t (c i) -> p c t i", i=4))

        def quantise(src, width, nm, bufs):
            codes = sb.tile([P, width], U32, name=nm + "_codes", bufs=bufs, align_bytes=64)
            scales = sb.tile([P, width], U8, name=nm + "_scales", bufs=bufs, align_bytes=64)
            nc.vector.quantize_mx(out=codes[:].bitcast(FP8X4), scales=scales[:], in_=src)
            return codes, scales

        xq, rq, lq, zq, qq, adjq = {}, {}, {}, {}, {}, {}

        def quant_x(b, g):
            xq[b, g] = quantise(mixed["x", b, g][:].rearrange("p f t -> p (f t)"), F, "xq", 4)

        def quant_r(b):
            rq[b] = quantise(mixed["r", b][:].rearrange("p c t -> p (c t)"), G * C, "rq", 2)

        def quant_l(b):
            lq[b] = quantise(mixed["l", b][:].rearrange("p c t -> p (c t)"), G * C, "lq", 2)

        adj_bf, adj_t, turned = {}, {}, {}

        def scale_adj(i):
            adj_bf[i] = sb.tile([P, N], BF16, name="adj_bf", bufs=6, align_bytes=64)
            nc.vector.tensor_tensor(out=adj_bf[i][:], in0=adj_raw[i // R, i // T % G][:, i % T, :].bitcast(FP8),
                                    in1=scale_row[:], op=ALU.mult)

        def turn_tensor(i):
            words = adj_bf[i][:].bitcast(F32)
            turned[i] = ps.tile([P, G, 2, P], F32, name="turned", tag="tr", bufs=2)
            for g in range(G):
                for u in range(2):
                    nc.tensor.transpose(turned[i][:, g, u, :], words[:, 256 * g + u:256 * (g + 1):2], ident_f[:])

        def turn_out(i):
            if i // 2 not in adj_t:
                adj_t[i // 2] = sb.tile([P, 2 * G * P * T], BF16, name="adj_t", bufs=3, align_bytes=64)
            words = adj_t[i // 2][:].bitcast(F32)[:, i % 2 * 512:(i % 2 + 1) * 512]
            nc.scalar.copy(out=words.rearrange("p (g n u) -> p g n u", g=G, u=2),
                           in_=turned[i][:].rearrange("p g u n -> p g n u"))

        def turn(i):
            turn_tensor(i)
            turn_out(i)

        def quant_adj(j):
            adjq[j] = quantise(adj_t[j][:], 2 * G * P, "adjq", 4)

        def product(out, lhs, l0, rhs, r0, width, g):
            nc.tensor.matmul_mx(out=out, lhsT=lhs[0][:, l0:l0 + P].bitcast(FP8X4), lhsT_scale=lhs[1][:, l0:l0 + P],
                                rhs=rhs[0][:, r0:r0 + width].bitcast(FP8X4), rhs_scale=rhs[1][:, r0:r0 + width],
                                start=g == 0, stop=g == G - 1)

        sums, gelus, z_mixed, q_sums, q_mixed = {}, {}, {}, {}, {}

        def feat_tensor(i):
            sums[i] = ps.tile([P, F], F32, name="sums", bufs=2)
            for g in range(G):
                product(sums[i][:], adjq[i // 2], i % 2 * 256 + g * P, xq[i // R, g], 0, F, g)

        def feat_out(i):
            if i // T not in gelus:
                gelus[i // T] = sb.tile([P, T, F], F32, name="gelus", bufs=2, align_bytes=64)
            nc.scalar.activation(out=gelus[i // T][:, i % T, :], in_=sums[i][:], func=ACT.Gelu)

        def feat(i):
            feat_tensor(i)
            feat_out(i)

        def gain_z(u):
            z_mixed[u] = sb.tile([P, F, T], BF16, name="z_mixed", bufs=2, align_bytes=64)
            gain = gain_o[:, u % G * T:(u % G + 1) * T].unsqueeze(1).unsqueeze(3)
            nc.vector.tensor_tensor(out=z_mixed[u][:].rearrange("p (f i) t -> p f t i", i=4),
                                    in0=gelus[u][:].rearrange("p t (f i) -> p f t i", i=4),
                                    in1=gain.to_broadcast([P, F // 4, T, 4]), op=ALU.mult)

        def quant_z(u):
            zq[u // G, u % G] = quantise(z_mixed[u][:].rearrange("p f t -> p (f t)"), F, "zq", 3)

        def clusters(u, h):
            q_sums[u, h] = ps.tile([P, T, P], F32, name="q_sums", bufs=2)
            for t in range(T):
                for g in range(G):
                    product(q_sums[u, h][:, t, :], adjq[2 * u + t // 2], t % 2 * 256 + g * P, rq[u // G], g * C + h * P, P, g)

        def gain_q(u, h):
            if u not in q_mixed:
                q_mixed[u] = sb.tile([P, C, T], BF16, name="q_mixed", bufs=2, align_bytes=64)
            gain = gain_o[:, u % G * T:(u % G + 1) * T].unsqueeze(1)
            nc.vector.tensor_tensor(out=q_mixed[u][:, h * P:(h + 1) * P, :], in0=q_sums[u, h][:].rearrange("p t c -> p c t"),
                                    in1=gain.to_broadcast([P, P, T]), op=ALU.mult)

        def quant_q(u):
            qq[u // G, u % G] = quantise(q_mixed[u][:].rearrange("p c t -> p (c t)"), C, "qq", 3)

        def pool(engine, name, b, h):
            width, rhs, out = {"x": (F, zq, out_0), "a": (C, qq, out_1)}[name]
            pooled = ps.tile([P, width], F32, name="pooled_" + name, tag="po", bufs=2)
            for g in range(G):
                product(pooled[:], lq[b], g * C + h * P, rhs[b, g], 0, width, g)
            result = sb.tile([P, width], F32, name="result_" + name, bufs=2, align_bytes=64)
            if engine == "scalar":
                nc.scalar.copy(out=result[:], in_=pooled[:])
            else:
                nc.vector.tensor_copy(out=result[:], in_=pooled[:])
            nc.sync.dma_start(out=out[b, h * P:(h + 1) * P, :], in_=result[:])

        load_logits(0, 1)
        load_scale()
        load_logits(0, 0)
        spread_scale(1)
        spread_scale(0)
        max_first(0, 1)
        max_first(0, 0)
        max_half(0, 64)
        load_logits(1, 1)
        max_first(1, 1)
        load_logits(1, 0)
        gather_scale(1)
        load_adj(0, 0, 0)
        load_gain("gr")
        max_half(0, 32)
        max_first(1, 0)
        gather_scale(0)
        max_last(0)
        max_half(1, 64)
        scale_adj(0)
        max_half(1, 32)
        load_adj(0, 0, 1)
        load_x(0, 1)
        scale_adj(2)
        exps(0, 0)
        load_gain("gl")
        max_last(1)
        exps(0, 1)
        scale_adj(1)
        widen_gain("gr")
        exps(1, 0)
        scale_adj(3)
        invert(0)
        widen_gain("gl")
        slopes(0)
        exps(1, 1)
        turn(0)
        load_adj(0, 1, 0)
        scale_adj(5)
        assign("scalar", "l", 0, 1, (3,))
        assign("vector", "r", 0, 1, (2,))
        invert(1)
        load_adj(0, 1, 1)
        assign("vector", "l", 0, 1, (0,))
        load_x(0, 0)
        load_adj(1, 0, 0)
        scale_adj(4)
        assign("scalar", "r", 0, 1, (1,))
        mix("tensor", ("x", 0, 1), 0)
        turn(2)
        assign("scalar", "r", 0, 1, (0,))
        load_gain("go")
        assign("scalar", "l", 0, 1, (1,))
        mix("tensor", ("x", 0, 1), 1)
        scale_adj(6)
        assign("vector", "r", 0, 0, (1,))
        scale_adj(7)
        assign("scalar", "r", 0, 0, (0,))
        turn(3)
        mix_tensor(("x", 0, 0), 1)
        assign("vector", "r", 0, 0, (3,))
        slopes(1)
        assign("scalar", "r", 0, 1, (3,))
        turn(1)
        quant_adj(1)
        quant_x(0, 1)
        mix_out(("x", 0, 0), 1)
        load_x(1, 0)
        assign("scalar", "r", 0, 0, (2,))
        mix("tensor", ("x", 0, 0), 0)
        turn(4)
        quant_adj(0)
        load_adj(1, 0, 1)
        turn(5)
        mix("vector", ("r", 0), 1)
        widen_gain("go")
        quant_x(0, 0)
        scale_adj(8)
        assign("vector", "l", 0, 0, (3,))
        quant_adj(2)
        load_adj(1, 1, 0)
        load_adj(1, 1, 1)
        assign("scalar", "r", 1, 1, (0,))
        assign("scalar", "l", 0, 0, (1,))
        mix("tensor", ("r", 0), 0)
        assign("scalar", "r", 1, 1, (3,))
        turn(6)
        turn(7)
        scale_adj(10)
        feat(0)
        quant_r(0)
        scale_adj(9)
        feat(3)
        mix_tensor(("x", 1, 0), 1)
        turn_tensor(8)
        load_x(1, 1)
        assign("scalar", "r", 1, 1, (2,))
        scale_adj(11)
        turn_tensor(10)
        clusters(0, 0)
        quant_adj(3)
        assign("scalar", "l", 0, 0, (2,))
        mix("scalar", ("x", 1, 0), 0)
        feat(1)
        assign("scalar", "l", 0, 1, (2,))
        clusters(1, 0)
        scale_adj(13)
        mix("vector", ("x", 1, 1), 1)
        gain_q(0, 0)
        mix("scalar", ("x", 1, 1), 0)
        feat(2)
        gain_q(1, 0)
        assign("vector", "l", 1, 0, (3,))
        scale_adj(12)
        assign("scalar", "r", 1, 0, (1,))
        turn_out(8)
        assign("scalar", "r", 1, 0, (2,))
        turn_out(10)
        feat(4)
        clusters(1, 1)
        clusters(0, 1)
        feat_tensor(5)
        quant_x(1, 1)
        turn(11)
        gain_q(1, 1)
        gain_z(0)
        assign("vector", "r", 1, 0, (0,))
        gain_q(0, 1)
        scale_adj(14)
        feat_out(5)
        mix_out(("x", 1, 0), 1)
        quant_adj(5)
        assign("scalar", "r", 1, 1, (1,))
        assign("scalar", "r", 1, 0, (3,))
        turn(9)
        mix_tensor(("l", 0), 1)
        assign("scalar", "l", 0, 0, (0,))
        feat(6)
        quant_x(1, 0)
        mix("scalar", ("r", 1), 1)
        feat(7)
        quant_adj(4)
        scale_adj(15)
        quant_z(0)
        mix_out(("l", 0), 1)
        turn(12)
        turn(14)
        gain_z(1)
        mix_tensor(("r", 1), 0)
        feat(8)
        mix_out(("r", 1), 0)
        feat(10)
        turn(13)
        mix("vector", ("l", 0), 0)
        turn_tensor(15)
        quant_r(1)
        assign("vector", "l", 1, 0, (2,))
        quant_z(1)
        quant_q(0)
        quant_adj(6)
        quant_q(1)
        assign("scalar", "l", 1, 1, (2,))
        feat(9)
        turn_out(15)
        feat(11)
        clusters(2, 0)
        quant_adj(7)
        quant_l(0)
        assign("scalar", "l", 1, 1, (0,))
        assign("scalar", "l", 1, 0, (0,))
        feat(12)
        assign("scalar", "l", 1, 1, (3,))
        feat(13)
        gain_z(2)
        gain_q(2, 0)
        assign("scalar", "l", 1, 0, (1,))
        pool("scalar", "x", 0, 0)
        feat(14)
        feat(15)
        quant_z(2)
        assign("scalar", "l", 1, 1, (1,))
        pool("scalar", "x", 0, 1)
        clusters(3, 0)
        gain_z(3)
        gain_q(3, 0)
        mix("scalar", ("l", 1), 1)
        mix("tensor", ("l", 1), 0)
        clusters(2, 1)
        pool("scalar", "a", 0, 1)
        quant_l(1)
        pool("scalar", "a", 0, 0)
        clusters(3, 1)
        quant_z(3)
        pool("scalar", "x", 1, 0)
        pool("scalar", "x", 1, 1)
        gain_q(2, 1)
        gain_q(3, 1)
        quant_q(2)
        quant_q(3)
        pool("vector", "a", 1, 1)
        pool("vector", "a", 1, 0)
